import numpy as np
CORES = [52,180,308,436]
N = 4
PERM = [[0,1],[1,2],[2,3],[3,0]]
def setup_inputs(rng):
    return {"x": rng.standard_normal((N, 128, 1024), dtype=np.float32)}
def reference(x):
    y = np.empty_like(x)
    for s, d in PERM:
        y[d] = x[s]
    return {"y": y}

@@ -1,0 +1,78 @@
+import concourse.bass as bass
+
+ROUNDS = 2
+WAYS = 4
+UNITS = WAYS * ROUNDS
+NCOL = 1024 // UNITS
+XROWS = 128 // UNITS
+
+SCRATCH = {
+    "stage": ("dram", [UNITS, 128, NCOL], "float32"),
+    "land": ("dram", [UNITS, 128, NCOL], "float32"),
+}
+SEMAPHORES = (["stored", "sent"]
+              + ["l%d" % r for r in range(ROUNDS)]
+              + ["h%d" % r for r in range(ROUNDS)]
+              + ["a%d" % r for r in range(ROUNDS)])
+
+SEND_MASKS = [0x000F, 0x00F0, 0x0F00, 0xF000]
+SEND_ENG = 4
+HELP_MASK, HELP_ENG = 0x00FF, 8
+
+
+def helpers_of(core):
+    base = core - core % 8
+    return [base + 2 * q for q in range(4) if q != (core % 8) // 2]
+
+
+def sem(T, name):
+    return {"h0": T.sem.h0, "h1": T.sem.h1, "a0": T.sem.a0, "a1": T.sem.a1, "l0": T.sem.l0, "l1": T.sem.l1}[name]
+
+
+def rank_program(g, core, T, topo):
+    perm = T.tables["PERM"]
+    cores = T.cores
+    rank = T.rank_of(core)
+
+    if rank is None:
+        for s, d in perm:
+            src, dst = cores[s], cores[d]
+            hs = helpers_of(src)
+            if s != d and core in hs:
+                w = 1 + hs.index(core)
+                rid, pid = topo.addr(dst, core)
+                for r in range(ROUNDS):
+                    t = WAYS * r + w
+                    g.wait_ge(sem(T, "h%d" % r), SEND_ENG)
+                    g.remote_dma(T.land[t], T.stage[t], sem(T, "a%d" % r), T.sem.sent, pid, rid, HELP_MASK)
+                g.wait_ge(T.sem.sent, HELP_ENG * ROUNDS)
+        return
+
+    dst = [cores[d] for s, d in perm if s == rank][0]
+    rr = WAYS * XROWS
+    if dst == core:
+        g.dma_start(T.stage[:], T.x[:]).then_inc(T.sem.l0, 16)
+        g.wait_ge(T.sem.l0, 16)
+        g.dma_start(T.y[:], T.stage[:]).then_inc(T.sem.stored, 16)
+        g.wait_ge(T.sem.stored, 16)
+        return
+
+    ways = [dst] + helpers_of(core)
+    for r in range(ROUNDS):
+        g.dma_start(T.stage[WAYS * r:WAYS * (r + 1)], T.x[rr * r:rr * (r + 1), :]).then_inc(sem(T, "l%d" % r), 16)
+    for r in range(ROUNDS):
+        g.wait_ge(sem(T, "l%d" % r), 16)
+        trs = []
+        for w, to in enumerate(ways):
+            t = WAYS * r + w
+            rid, pid = topo.addr(to, core)
+            trs.append(bass.RemoteDMATransfer(
+                dst_ids=[bass.DstId(rid=rid, pnc=pid)], dma_engine_mask=SEND_MASKS[w],
+                remote_sem=sem(T, ("a%d" if w == 0 else "h%d") % r),
+                src=T.stage[t], dst=(T.land[t] if w == 0 else T.stage[t])))
+        g.remote_dma_fused(trs, local_sem=T.sem.sent)
+    for r in range(ROUNDS):
+        g.wait_ge(sem(T, "a%d" % r), SEND_ENG + HELP_ENG * (WAYS - 1))
+        g.dma_start(T.y[rr * r:rr * (r + 1), :], T.land[WAYS * r:WAYS * (r + 1)]).then_inc(T.sem.stored, 16)
+    g.wait_ge(T.sem.stored, 16 * ROUNDS)
+    g.wait_ge(T.sem.sent, SEND_ENG * WAYS * ROUNDS)

@@ -1,78 +1,117 @@
 import concourse.bass as bass
 
-ROUNDS = 2
-WAYS = 4
-UNITS = WAYS * ROUNDS
-NCOL = 1024 // UNITS
-XROWS = 128 // UNITS
-
-SCRATCH = {
-    "stage": ("dram", [UNITS, 128, NCOL], "float32"),
-    "land": ("dram", [UNITS, 128, NCOL], "float32"),
+HE = 8
+PLAN = {
+    "S": [(128, [(0, 0x000F), (1, 0x00F0), (2, 0x0F00), (3, 0xF000)]),
+          (128, [(0, 0x000F), (1, 0x00F0), (2, 0x0F00), (3, 0xF000)])],
+    "C": [(32, [(4 + i, 1 << i) for i in range(8)]),
+          (96, [(0, 0x000F), (1, 0x00F0), (2, 0x0F00), (3, 0xF000)]),
+          (96, [(0, 0x000F), (1, 0x00F0), (2, 0x0F00), (3, 0xF000)])],
 }
+STORE = {"S": [0, 1], "C": [1, 2, 0]}
+NR = max(len(v) for v in PLAN.values())
+
+SCRATCH = {}
+for k_, v_ in PLAN.items():
+    for r_, (n_, us_) in enumerate(v_):
+        SCRATCH["b%s%d" % (k_, r_)] = ("dram", [len(us_), 128, n_], "float32")
 SEMAPHORES = (["stored", "sent"]
-              + ["l%d" % r for r in range(ROUNDS)]
-              + ["h%d" % r for r in range(ROUNDS)]
-              + ["a%d" % r for r in range(ROUNDS)])
-
-SEND_MASKS = [0x000F, 0x00F0, 0x0F00, 0xF000]
-SEND_ENG = 4
-HELP_MASK, HELP_ENG = 0x00FF, 8
+              + ["l%d" % r for r in range(NR)]
+              + ["h%d" % r for r in range(NR)]
+              + ["a%d" % r for r in range(NR)])
 
 
-def helpers_of(core):
-    base = core - core % 8
-    return [base + 2 * q for q in range(4) if q != (core % 8) // 2]
+def bits(m):
+    return bin(m).count("1")
 
 
-def sem(T, name):
-    return {"h0": T.sem.h0, "h1": T.sem.h1, "a0": T.sem.a0, "a1": T.sem.a1, "l0": T.sem.l0, "l1": T.sem.l1}[name]
+def routes(src, dst, topo):
+    base, me = src - src % 8, src % 8
+    rts = [[src, dst]] + [[src, base + 2 * q, dst] for q in range(4) if q != me // 2]
+    if topo.rack(topo.host(src)) == topo.rack(topo.host(dst)):
+        return "S", rts
+    for c in ((topo.chip(src) + 2) % 16, (topo.chip(src) - 2) % 16):
+        for q in range(4):
+            rts.append([src, topo.host(src) * 128 + c * 8 + 2 * q, topo.host(dst) * 128 + c * 8 + 2 * q, dst])
+    return "C", rts
+
+
+def names(T):
+    S = T.sem
+    return {
+        "l": [lambda: S.l0, lambda: S.l1, lambda: S.l2, lambda: S.l3, lambda: S.l4, lambda: S.l5],
+        "h": [lambda: S.h0, lambda: S.h1, lambda: S.h2, lambda: S.h3, lambda: S.h4, lambda: S.h5],
+        "a": [lambda: S.a0, lambda: S.a1, lambda: S.a2, lambda: S.a3, lambda: S.a4, lambda: S.a5],
+        "S": [lambda: T.bS0, lambda: T.bS1, lambda: T.bS2, lambda: T.bS3, lambda: T.bS4, lambda: T.bS5],
+        "C": [lambda: T.bC0, lambda: T.bC1, lambda: T.bC2, lambda: T.bC3, lambda: T.bC4, lambda: T.bC5],
+    }
+
+
+def relay_masks(k):
+    e = HE // k
+    return [((1 << e) - 1) << (e * i) for i in range(k)]
+
+
+def rows_of(kind):
+    out = [0]
+    for n, us in PLAN[kind]:
+        out.append(out[-1] + n * len(us) // 8)
+    return out
 
 
 def rank_program(g, core, T, topo):
     perm = T.tables["PERM"]
     cores = T.cores
     rank = T.rank_of(core)
+    N = names(T)
+
+    def send(kind, r, items, to, last):
+        rid, pid = topo.addr(to, core)
+        return [bass.RemoteDMATransfer(
+            dst_ids=[bass.DstId(rid=rid, pnc=pid)], dma_engine_mask=m, remote_sem=N["a" if last else "h"][r](),
+            src=N[kind][r]()[i], dst=N[kind][r]()[i]) for i, m in items]
 
     if rank is None:
         for s, d in perm:
-            src, dst = cores[s], cores[d]
-            hs = helpers_of(src)
-            if s != d and core in hs:
-                w = 1 + hs.index(core)
-                rid, pid = topo.addr(dst, core)
-                for r in range(ROUNDS):
-                    t = WAYS * r + w
-                    g.wait_ge(sem(T, "h%d" % r), SEND_ENG)
-                    g.remote_dma(T.land[t], T.stage[t], sem(T, "a%d" % r), T.sem.sent, pid, rid, HELP_MASK)
-                g.wait_ge(T.sem.sent, HELP_ENG * ROUNDS)
+            kind, rts = routes(cores[s], cores[d], topo)
+            for w, rt in enumerate(rts):
+                if core not in rt[1:-1]:
+                    continue
+                j = rt.index(core)
+                total = 0
+                for r, (n, us) in enumerate(PLAN[kind]):
+                    mine = [(i, m) for i, (ww, m) in enumerate(us) if ww == w]
+                    if not mine:
+                        continue
+                    g.wait_ge(N["h"][r](), sum(bits(m) for i, m in mine) if j == 1 else HE)
+                    hm = relay_masks(len(mine))
+                    g.remote_dma_fused(send(kind, r, [(i, hm[q]) for q, (i, m) in enumerate(mine)], rt[j + 1],
+                                            j + 2 == len(rt)), local_sem=T.sem.sent)
+                    total += HE
+                g.wait_ge(T.sem.sent, total)
         return
 
-    dst = [cores[d] for s, d in perm if s == rank][0]
-    rr = WAYS * XROWS
-    if dst == core:
-        g.dma_start(T.stage[:], T.x[:]).then_inc(T.sem.l0, 16)
-        g.wait_ge(T.sem.l0, 16)
-        g.dma_start(T.y[:], T.stage[:]).then_inc(T.sem.stored, 16)
-        g.wait_ge(T.sem.stored, 16)
-        return
+    ks, rts = [routes(cores[s], cores[d], topo) for s, d in perm if s == rank][0]
+    kr = [routes(cores[s], cores[d], topo) for s, d in perm if d == rank][0][0]
+    if ks == kr:
+        raise ValueError("a rank must send and receive over different kinds of link")
 
-    ways = [dst] + helpers_of(core)
-    for r in range(ROUNDS):
-        g.dma_start(T.stage[WAYS * r:WAYS * (r + 1)], T.x[rr * r:rr * (r + 1), :]).then_inc(sem(T, "l%d" % r), 16)
-    for r in range(ROUNDS):
-        g.wait_ge(sem(T, "l%d" % r), 16)
+    rows = rows_of(ks)
+    for r in range(len(PLAN[ks])):
+        g.dma_start(N[ks][r]()[:], T.x[rows[r]:rows[r + 1], :]).then_inc(N["l"][r](), 16)
+    total = 0
+    for r, (n, us) in enumerate(PLAN[ks]):
+        g.wait_ge(N["l"][r](), 16)
         trs = []
-        for w, to in enumerate(ways):
-            t = WAYS * r + w
-            rid, pid = topo.addr(to, core)
-            trs.append(bass.RemoteDMATransfer(
-                dst_ids=[bass.DstId(rid=rid, pnc=pid)], dma_engine_mask=SEND_MASKS[w],
-                remote_sem=sem(T, ("a%d" if w == 0 else "h%d") % r),
-                src=T.stage[t], dst=(T.land[t] if w == 0 else T.stage[t])))
+        for i, (w, m) in enumerate(us):
+            trs += send(ks, r, [(i, m)], rts[w][1], w == 0)
+            total += bits(m)
         g.remote_dma_fused(trs, local_sem=T.sem.sent)
-    for r in range(ROUNDS):
-        g.wait_ge(sem(T, "a%d" % r), SEND_ENG + HELP_ENG * (WAYS - 1))
-        g.dma_start(T.y[rr * r:rr * (r + 1), :], T.land[WAYS * r:WAYS * (r + 1)]).then_inc(T.sem.stored, 16)
-    g.wait_ge(T.sem.stored, 16 * ROUNDS)
-    g.wait_ge(T.sem.sent, SEND_ENG * WAYS * ROUNDS)
+    rows = rows_of(kr)
+    for r in STORE[kr]:
+        n, us = PLAN[kr][r]
+        cnt = sum(bits(m) for w, m in us if w == 0) + HE * len(set(w for w, m in us if w != 0))
+        g.wait_ge(N["a"][r](), cnt)
+        g.dma_start(T.y[rows[r]:rows[r + 1], :], N[kr][r]()[:]).then_inc(T.sem.stored, 16)
+    g.wait_ge(T.sem.stored, 16 * len(PLAN[kr]))
+    g.wait_ge(T.sem.sent, total)

@@ -39,11 +39,11 @@ def routes(src, dst, topo):
 def names(T):
     S = T.sem
     return {
-        "l": [lambda: S.l0, lambda: S.l1, lambda: S.l2, lambda: S.l3, lambda: S.l4, lambda: S.l5],
-        "h": [lambda: S.h0, lambda: S.h1, lambda: S.h2, lambda: S.h3, lambda: S.h4, lambda: S.h5],
-        "a": [lambda: S.a0, lambda: S.a1, lambda: S.a2, lambda: S.a3, lambda: S.a4, lambda: S.a5],
-        "S": [lambda: T.bS0, lambda: T.bS1, lambda: T.bS2, lambda: T.bS3, lambda: T.bS4, lambda: T.bS5],
-        "C": [lambda: T.bC0, lambda: T.bC1, lambda: T.bC2, lambda: T.bC3, lambda: T.bC4, lambda: T.bC5],
+        "l": [lambda: S.l0, lambda: S.l1, lambda: S.l2],
+        "h": [lambda: S.h0, lambda: S.h1, lambda: S.h2],
+        "a": [lambda: S.a0, lambda: S.a1, lambda: S.a2],
+        "S": [lambda: T.bS0, lambda: T.bS1],
+        "C": [lambda: T.bC0, lambda: T.bC1, lambda: T.bC2],
     }
 
 

import concourse.bass as bass

HE = 8
PLAN = {
    "S": [(128, [(0, 0x000F), (1, 0x00F0), (2, 0x0F00), (3, 0xF000)]),
          (128, [(0, 0x000F), (1, 0x00F0), (2, 0x0F00), (3, 0xF000)])],
    "C": [(32, [(4 + i, 1 << i) for i in range(8)]),
          (96, [(0, 0x000F), (1, 0x00F0), (2, 0x0F00), (3, 0xF000)]),
          (96, [(0, 0x000F), (1, 0x00F0), (2, 0x0F00), (3, 0xF000)])],
}
STORE = {"S": [0, 1], "C": [1, 2, 0]}
NR = max(len(v) for v in PLAN.values())

SCRATCH = {}
for k_, v_ in PLAN.items():
    for r_, (n_, us_) in enumerate(v_):
        SCRATCH["b%s%d" % (k_, r_)] = ("dram", [len(us_), 128, n_], "float32")
SEMAPHORES = (["stored", "sent"]
              + ["l%d" % r for r in range(NR)]
              + ["h%d" % r for r in range(NR)]
              + ["a%d" % r for r in range(NR)])


def bits(m):
    return bin(m).count("1")


def routes(src, dst, topo):
    base, me = src - src % 8, src % 8
    rts = [[src, dst]] + [[src, base + 2 * q, dst] for q in range(4) if q != me // 2]
    if topo.rack(topo.host(src)) == topo.rack(topo.host(dst)):
        return "S", rts
    for c in ((topo.chip(src) + 2) % 16, (topo.chip(src) - 2) % 16):
        for q in range(4):
            rts.append([src, topo.host(src) * 128 + c * 8 + 2 * q, topo.host(dst) * 128 + c * 8 + 2 * q, dst])
    return "C", rts


def names(T):
    S = T.sem
    return {
        "l": [lambda: S.l0, lambda: S.l1, lambda: S.l2],
        "h": [lambda: S.h0, lambda: S.h1, lambda: S.h2],
        "a": [lambda: S.a0, lambda: S.a1, lambda: S.a2],
        "S": [lambda: T.bS0, lambda: T.bS1],
        "C": [lambda: T.bC0, lambda: T.bC1, lambda: T.bC2],
    }


def relay_masks(k):
    e = HE // k
    return [((1 << e) - 1) << (e * i) for i in range(k)]


def rows_of(kind):
    out = [0]
    for n, us in PLAN[kind]:
        out.append(out[-1] + n * len(us) // 8)
    return out


def rank_program(g, core, T, topo):
    perm = T.tables["PERM"]
    cores = T.cores
    rank = T.rank_of(core)
    N = names(T)

    def send(kind, r, items, to, last):
        rid, pid = topo.addr(to, core)
        return [bass.RemoteDMATransfer(
            dst_ids=[bass.DstId(rid=rid, pnc=pid)], dma_engine_mask=m, remote_sem=N["a" if last else "h"][r](),
            src=N[kind][r]()[i], dst=N[kind][r]()[i]) for i, m in items]

    if rank is None:
        for s, d in perm:
            kind, rts = routes(cores[s], cores[d], topo)
            for w, rt in enumerate(rts):
                if core not in rt[1:-1]:
                    continue
                j = rt.index(core)
                total = 0
                for r, (n, us) in enumerate(PLAN[kind]):
                    mine = [(i, m) for i, (ww, m) in enumerate(us) if ww == w]
                    if not mine:
                        continue
                    g.wait_ge(N["h"][r](), sum(bits(m) for i, m in mine) if j == 1 else HE)
                    hm = relay_masks(len(mine))
                    g.remote_dma_fused(send(kind, r, [(i, hm[q]) for q, (i, m) in enumerate(mine)], rt[j + 1],
                                            j + 2 == len(rt)), local_sem=T.sem.sent)
                    total += HE
                g.wait_ge(T.sem.sent, total)
        return

    ks, rts = [routes(cores[s], cores[d], topo) for s, d in perm if s == rank][0]
    kr = [routes(cores[s], cores[d], topo) for s, d in perm if d == rank][0][0]
    if ks == kr:
        raise ValueError("a rank must send and receive over different kinds of link")

    rows = rows_of(ks)
    for r in range(len(PLAN[ks])):
        g.dma_start(N[ks][r]()[:], T.x[rows[r]:rows[r + 1], :]).then_inc(N["l"][r](), 16)
    total = 0
    for r, (n, us) in enumerate(PLAN[ks]):
        g.wait_ge(N["l"][r](), 16)
        trs = []
        for i, (w, m) in enumerate(us):
            trs += send(ks, r, [(i, m)], rts[w][1], w == 0)
            total += bits(m)
        g.remote_dma_fused(trs, local_sem=T.sem.sent)
    rows = rows_of(kr)
    for r in STORE[kr]:
        n, us = PLAN[kr][r]
        cnt = sum(bits(m) for w, m in us if w == 0) + HE * len(set(w for w, m in us if w != 0))
        g.wait_ge(N["a"][r](), cnt)
        g.dma_start(T.y[rows[r]:rows[r + 1], :], N[kr][r]()[:]).then_inc(T.sem.stored, 16)
    g.wait_ge(T.sem.stored, 16 * len(PLAN[kr]))
    g.wait_ge(T.sem.sent, total)
